import numpy as np
import ml_dtypes


def mxq(x, axis, fmt="e4m3"):
    dtype, down = {"e4m3": (ml_dtypes.float8_e4m3fn, 7), "e5m2": (ml_dtypes.float8_e5m2, 14)}[fmt]
    v = np.moveaxis(np.asarray(x, np.float32).astype(ml_dtypes.bfloat16).astype(np.float64), axis, -1)
    blocks = v.reshape(v.shape[:-1] + (-1, 32))
    amax = np.abs(blocks).max(-1, keepdims=True)
    byte = np.maximum(np.where(amax > 0, np.frexp(amax)[1] - 1 + 127, 0) - down, 1)
    scale = np.exp2(byte - 127.0)
    codes = (blocks / scale).astype(np.float32).astype(dtype).astype(np.float64)
    return np.moveaxis((codes * scale).reshape(v.shape), -1, axis)


WIDE = False


def mx_kscale(k):
    if not WIDE:
        return np.ones(k)
    levels = np.array([30, -30])
    if k % 512:
        return np.exp2(np.random.permutation(np.resize(levels, k // 32))).repeat(32)
    a = np.empty((k // 512, 16))
    for p in range(k // 512):
        a[p, :8] = np.random.permutation(np.resize(levels, 8))
        for g in range(8):
            far = levels[np.abs(levels - a[p, g]) >= 10]
            a[p, g + 8] = far[np.random.randint(len(far))]
    return np.exp2(a.ravel()).repeat(32)


def f64(x):
    return np.asarray(x).astype(np.float64)


def striped(idx):
    return np.tile(np.asarray(idx).reshape(-1, 16).T, (8, 1)).astype(np.uint16)


def unstriped(offs):
    return offs[:16].T.reshape(-1).astype(np.int64)


E2M1 = np.array([0.0, 0.5, 1.0, 1.5, 2.0, 3.0, 4.0, 6.0, -0.0, -0.5, -1.0, -1.5, -2.0, -3.0, -4.0, -6.0])


def pack_weight(w, fmt):
    k, n = w.shape
    w = f64(np.asarray(w, np.float32).astype(ml_dtypes.bfloat16)).reshape(k // 32, 32, n)
    amax = np.abs(w).max(1)
    if fmt in ("e4m3", "e5m2"):
        byte = np.frexp(amax)[1] - 1 + 127 - (7 if fmt == "e4m3" else 14)
    else:
        mant, ex = np.frexp(amax / 6.0)
        byte = np.where(mant > 0.5, ex, ex - 1) + 127
    byte = np.clip(np.where(amax > 0, byte, 1), 1, 254)
    scaled = (w * np.exp2(127.0 - byte)[:, None, :]).reshape(k, n).astype(np.float32)
    by_word = np.ascontiguousarray(scaled.reshape(k // 512, 128, 4, n).transpose(0, 1, 3, 2))
    if fmt in ("e4m3", "e5m2"):
        words = by_word.astype(ml_dtypes.float8_e4m3fn if fmt == "e4m3" else ml_dtypes.float8_e5m2).view(np.uint8)
    else:
        c = by_word.astype(ml_dtypes.float4_e2m1fn).view(np.uint8) & 0xF
        words = (c[..., 0::2] | (c[..., 1::2] << 4)).reshape(k // 512, 128, 2 * n)
    return np.ascontiguousarray(words), np.ascontiguousarray(byte.astype(np.uint8).reshape(k // 512, 16, n))


def unpack_weight(words, scales, fmt):
    g, _, n = scales.shape
    words = np.ascontiguousarray(words).reshape(g, 128, n, -1)
    if fmt in ("e4m3", "e5m2"):
        vals = words.view(ml_dtypes.float8_e4m3fn if fmt == "e4m3" else ml_dtypes.float8_e5m2).astype(np.float64)
    else:
        nib = np.empty((g, 128, n, 4), np.uint8)
        nib[..., 0::2] = words & 0xF
        nib[..., 1::2] = words >> 4
        vals = E2M1[nib]
    vals = vals * np.repeat(np.exp2(scales.astype(np.float64) - 127.0), 8, axis=1)[..., None]
    return vals.transpose(0, 1, 3, 2).reshape(g * 512, n)


K, F, T, Z, J, R, C, D, N = 512, 512, 1024, 1024, 256, 512, 512, 512, 256


def setup_inputs():
    n = np.random.standard_normal
    idx = np.random.permutation(T)[:J]
    idx2 = np.random.permutation(Z)[:J]
    idx3 = np.random.permutation(C)[:J]
    idx4 = np.random.permutation(D)[:J]
    idx5 = np.random.permutation(C)[:J]
    idx6 = np.random.permutation(D)[:J]
    fk = mx_kscale(K)
    fr = mx_kscale(R)
    ff = mx_kscale(F)
    xtp = pack_weight(n((K, T)) / fk[:, None], "e4m3")
    wp = pack_weight(n((K, R)) * 1 / np.sqrt(K) * fk[:, None] * fr, "e2m1")
    xop = pack_weight(n((F, Z)) / ff[:, None], "e2m1")
    w2p = pack_weight(n((F, R)) * 1 / np.sqrt(F) * ff[:, None] * fr, "e5m2")
    wbp = pack_weight(n((R, N)) * 1 / np.sqrt(R) / fr[:, None], "e5m2")
    return {
        "xt_words": xtp[0],
        "xt_scales": xtp[1],
        "w_words": wp[0],
        "w_scales": wp[1],
        "xo_words": xop[0],
        "xo_scales": xop[1],
        "w2_words": w2p[0],
        "w2_scales": w2p[1],
        "wb_words": wbp[0],
        "wb_scales": wbp[1],
        "offs": striped(idx),
        "offs2": striped(idx2),
        "offs3": striped(idx3),
        "offs4": striped(idx4),
        "offs5": striped(idx5),
        "offs6": striped(idx6),
    }


def reference(xt_words, xt_scales, w_words, w_scales, xo_words, xo_scales, w2_words, w2_scales, wb_words, wb_scales, offs, offs2, offs3, offs4, offs5, offs6):
    idx = unstriped(offs)
    idx2 = unstriped(offs2)
    idx3 = unstriped(offs3)
    idx4 = unstriped(offs4)
    idx5 = unstriped(offs5)
    idx6 = unstriped(offs6)
    xtu = unpack_weight(xt_words, xt_scales, "e4m3")
    wu = unpack_weight(w_words, w_scales, "e2m1")
    xou = unpack_weight(xo_words, xo_scales, "e2m1")
    w2u = unpack_weight(w2_words, w2_scales, "e5m2")
    wbu = unpack_weight(wb_words, wb_scales, "e5m2")
    xtidxg = xtu[:, idx]
    a = wu.T @ xtidxg
    xoidx2g = xou[:, idx2]
    b = w2u.T @ xoidx2g
    pw = np.zeros((R, C))
    pw[:, idx3] = a
    pv = np.zeros((R, D))
    pv[:, idx4] = b
    hid = np.maximum(pw[:, idx5] - b, pv[:, idx6] - a)
    hidq = mxq(hid, 0, "e4m3")
    y = wbu.T @ hidq
    return y

@@ -1,0 +1,184 @@
+from contextlib import ExitStack
+
+import concourse.mybir as mybir
+
+K, T, Z, J, R, C, N = 512, 1024, 1024, 256, 512, 512, 256
+FLOPS = 2 * K * R * J * 2 + 2 * R * N * J
+
+F32 = mybir.dt.float32
+BF16 = mybir.dt.bfloat16
+I32 = mybir.dt.int32
+U32 = mybir.dt.uint32
+U16 = mybir.dt.uint16
+U8 = mybir.dt.uint8
+E4M3 = mybir.dt.float8_e4m3fn_x4
+E5M2 = mybir.dt.float8_e5m2_x4
+E2M1 = mybir.dt.float4_e2m1fn_x4
+COPY = mybir.ActivationFunctionType.Copy
+SUB = mybir.AluOpType.subtract
+MAX = mybir.AluOpType.max
+
+P = 128
+PACK = 4
+
+
+def tile_list_crossread_twotab_one_plain_kernel(
+    tc, xt_words, xt_scales, w_words, w_scales, xo_words, xo_scales, w2_words, w2_scales,
+    wb_words, wb_scales, offs, offs2, offs3, offs4, offs5, offs6, out,
+):
+    nc = tc.nc
+    with ExitStack() as ctx:
+        keep = ctx.enter_context(tc.tile_pool(name="keep", bufs=1))
+        psum = ctx.enter_context(tc.psum_pool(name="psum", bufs=1))
+
+        def sb(name, width, dtype):
+            return keep.tile([P, width], dtype, name=name, align_bytes=64)
+
+        def load_list(name, src):
+            tile = keep.tile([P, J // 16], U16, name=name)
+            nc.sync.dma_start(tile[:], src)
+            return tile
+
+        def load_words(name, src, width, dtype):
+            tile = sb(name, width, dtype)
+            nc.sync.dma_start(tile[:].bitcast(I32), src.bitcast(I32))
+            return tile
+
+        def fp8_rows(words):
+            return words[0].rearrange("p n t -> p (n t)")
+
+        def staged_plane(name, n, memset_engine):
+            tile = sb(name, 2 * n, U8)
+            memset_engine.memset(tile[0:64, :].bitcast(I32), 0)
+            return tile
+
+        def load_staged(tile, scales, n, queue):
+            rows = scales[0].bitcast(I32).rearrange("(h g r) n -> g r h n", h=2, g=2)
+            for g in range(2):
+                queue.dma_start(
+                    tile[32 * g : 32 * g + 4, :].bitcast(I32).rearrange("r (h n) -> r h n", h=2), rows[g]
+                )
+
+        def lift_upper_half(tile, n):
+            nc.vector.tensor_copy(tile[64:128, 0:n].bitcast(I32), tile[0:64, n : 2 * n].bitcast(I32))
+
+        def unstage(name, tile, n):
+            plane = sb(name, n, U8)
+            for h in range(2):
+                nc.vector.tensor_copy(plane[64 * h : 64 * h + 64, :].bitcast(I32), tile[0:64, n * h : n * h + n].bitcast(I32))
+            return plane
+
+        def deal(engine_copy, name, src, dtype, run):
+            tile = sb(name, R, dtype)
+            engine_copy(
+                tile[:].rearrange("p (t c i) -> p c t i", t=PACK, i=run),
+                src.rearrange("p (c i t) -> p c t i", t=PACK, i=run),
+            )
+            return tile
+
+        xo_s = staged_plane("xo_s", Z, nc.vector)
+        w2_s = staged_plane("w2_s", R, nc.gpsimd)
+        xt_s = staged_plane("xt_s", T, nc.gpsimd)
+        w_s = staged_plane("w_s", R, nc.gpsimd)
+        wb_s = sb("wb_s", N, U8)
+        nc.gpsimd.memset(wb_s[:].bitcast(I32), 0)
+
+        o2 = load_list("o2", offs2)
+        xo_w = load_words("xo_w", xo_words[0], Z, U16)
+        w2_w = load_words("w2_w", fp8_rows(w2_words), R, U32)
+        w_w = load_words("w_w", w_words[0], R, U16)
+        load_staged(xo_s, xo_scales, Z, nc.scalar)
+        load_staged(w2_s, w2_scales, R, nc.scalar)
+        o4 = load_list("o4", offs4)
+        o1 = load_list("o1", offs)
+        load_staged(xt_s, xt_scales, T, nc.sync)
+        load_staged(w_s, w_scales, R, nc.sync)
+        xt_w = load_words("xt_w", fp8_rows(xt_words), T, U32)
+        o3 = load_list("o3", offs3)
+        o6 = load_list("o6", offs6)
+        o5 = load_list("o5", offs5)
+        wb_w = load_words("wb_w", fp8_rows(wb_words), N, U32)
+        for q in range(4):
+            nc.sync.dma_start(wb_s[32 * q : 32 * q + 4, :].bitcast(I32), wb_scales[0, 4 * q : 4 * q + 4, :].bitcast(I32))
+
+        banks = [psum.tile([P, 512], F32, name=f"bank{i}") for i in range(8)]
+
+        xo_p = unstage("xo_p", xo_s, Z)
+        xo_gs = sb("xo_gs", J, U8)
+        nc.vector.tensor_copy(xo_gs[:], xo_p[:].indirect(o2[:]))
+        lift_upper_half(w2_s, R)
+        w2_ds = deal(nc.vector.tensor_copy, "w2_ds", w2_s[:, 0:R], U8, 16)
+        xo_gw = sb("xo_gw", J, U16)
+        nc.vector.tensor_copy(xo_gw[:], xo_w[:].indirect(o2[:]))
+        w2_dw = deal(nc.scalar.copy, "w2_dw", w2_w[:], U32, 4)
+        w_dw = deal(nc.scalar.copy, "w_dw", w_w[:], U16, 8)
+
+        pv = [sb(f"pv{t}", C, F32) for t in range(PACK)]
+        pw = [sb(f"pw{t}", C, F32) for t in range(PACK)]
+        for t in range(PACK):
+            nc.vector.memset(pv[t][:], 0.0)
+
+        b_sb = [sb(f"b{t}", J, F32) for t in range(PACK)]
+        a_sb = [sb(f"a{t}", J, F32) for t in range(PACK)]
+        for t in range(PACK):
+            cols = slice(P * t, P * (t + 1))
+            nc.tensor.matmul_mx(
+                out=banks[t][:, 0:J], lhsT=w2_dw[:, cols].bitcast(E5M2), lhsT_scale=w2_ds[:, cols],
+                rhs=xo_gw[:].bitcast(E2M1), rhs_scale=xo_gs[:], start=True, stop=True,
+            )
+        nc.scalar.copy(b_sb[0][:], banks[0][:, 0:J])
+        for t in range(1, PACK):
+            nc.vector.tensor_copy(b_sb[t][:], banks[t][:, 0:J])
+        for t in range(PACK):
+            nc.scalar.activation(out=pv[t][:].indirect(o4[:]), in_=b_sb[t][:], func=COPY)
+
+        xt_p = unstage("xt_p", xt_s, T)
+        xt_gs = sb("xt_gs", J, U8)
+        nc.vector.tensor_copy(xt_gs[:], xt_p[:].indirect(o1[:]))
+        lift_upper_half(w_s, R)
+        w_ds = deal(nc.vector.tensor_copy, "w_ds", w_s[:, 0:R], U8, 16)
+        xt_gw = sb("xt_gw", J, U32)
+        nc.vector.tensor_copy(xt_gw[:], xt_w[:].indirect(o1[:]))
+        for t in range(PACK):
+            cols = slice(P * t, P * (t + 1))
+            nc.tensor.matmul_mx(
+                out=banks[PACK + t][:, 0:J], lhsT=w_dw[:, cols].bitcast(E2M1), lhsT_scale=w_ds[:, cols],
+                rhs=xt_gw[:].bitcast(E4M3), rhs_scale=xt_gs[:], start=True, stop=True,
+            )
+        for t in range(PACK):
+            nc.vector.memset(pw[t][:], 0.0)
+        for t in range(PACK):
+            nc.vector.tensor_copy(a_sb[t][:], banks[PACK + t][:, 0:J])
+        nc.vector.tensor_copy(pw[0][:].indirect(o3[:]), a_sb[0][:])
+        for t in range(1, PACK):
+            nc.scalar.activation(out=pw[t][:].indirect(o3[:]), in_=a_sb[t][:], func=COPY)
+
+        u = keep.tile([P, PACK, J], F32, name="u", align_bytes=64)
+        v = keep.tile([P, PACK, J], F32, name="v", align_bytes=64)
+        for t in range(PACK):
+            nc.vector.tensor_tensor(v[:, t, :], pv[t][:].indirect(o6[:]), a_sb[t][:], SUB)
+        for t in range(PACK):
+            nc.vector.tensor_tensor(u[:, t, :], pw[t][:].indirect(o5[:]), b_sb[t][:], SUB)
+
+        hid = keep.tile([P, J, PACK], BF16, name="hid", align_bytes=64)
+        nc.vector.tensor_tensor(
+            hid[:].rearrange("p (c i) t -> p c t i", i=4),
+            u[:].rearrange("p t (c i) -> p c t i", i=4),
+            v[:].rearrange("p t (c i) -> p c t i", i=4),
+            MAX,
+        )
+        hid_w = sb("hid_w", J, U32)
+        hid_s = sb("hid_s", J, U8)
+        nc.vector.quantize_mx(out=hid_w[:].bitcast(E4M3), scales=hid_s[:], in_=hid[:].rearrange("p j t -> p (j t)"))
+
+        for m in range(N // P):
+            cols = slice(P * m, P * (m + 1))
+            nc.tensor.matmul_mx(
+                out=banks[m][:, 0:J], lhsT=wb_w[:, cols].bitcast(E5M2), lhsT_scale=wb_s[:, cols],
+                rhs=hid_w[:].bitcast(E4M3), rhs_scale=hid_s[:], start=True, stop=True,
+            )
+        y = [sb(f"y{m}", J, F32) for m in range(N // P)]
+        nc.scalar.copy(y[0][:], banks[0][:, 0:J])
+        nc.vector.tensor_copy(y[1][:], banks[1][:, 0:J])
+        nc.scalar.dma_start(out[0:P, :], y[0][:])
+        nc.sync.dma_start(out[P : 2 * P, :], y[1][:])

@@ -47,26 +47,12 @@ def tile_list_crossread_twotab_one_plain_kernel(
         def fp8_rows(words):
             return words[0].rearrange("p n t -> p (n t)")
 
-        def staged_plane(name, n, memset_engine):
-            tile = sb(name, 2 * n, U8)
-            memset_engine.memset(tile[0:64, :].bitcast(I32), 0)
+        def load_plane(name, scales, n):
+            tile = sb(name, n, U8)
+            for q in range(4):
+                rows = scales[0, 4 * q : 4 * q + 4, :].bitcast(I32)
+                nc.sync.dma_start(tile[32 * q : 32 * q + 32, :].bitcast(I32), rows.unsqueeze(0).to_broadcast([8, 4, n // 4]))
             return tile
-
-        def load_staged(tile, scales, n, queue):
-            rows = scales[0].bitcast(I32).rearrange("(h g r) n -> g r h n", h=2, g=2)
-            for g in range(2):
-                queue.dma_start(
-                    tile[32 * g : 32 * g + 4, :].bitcast(I32).rearrange("r (h n) -> r h n", h=2), rows[g]
-                )
-
-        def lift_upper_half(tile, n):
-            nc.vector.tensor_copy(tile[64:128, 0:n].bitcast(I32), tile[0:64, n : 2 * n].bitcast(I32))
-
-        def unstage(name, tile, n):
-            plane = sb(name, n, U8)
-            for h in range(2):
-                nc.vector.tensor_copy(plane[64 * h : 64 * h + 64, :].bitcast(I32), tile[0:64, n * h : n * h + n].bitcast(I32))
-            return plane
 
         def deal(engine_copy, name, src, dtype, run):
             tile = sb(name, R, dtype)
@@ -76,47 +62,43 @@ def tile_list_crossread_twotab_one_plain_kernel(
             )
             return tile
 
-        xo_s = staged_plane("xo_s", Z, nc.vector)
-        w2_s = staged_plane("w2_s", R, nc.gpsimd)
-        xt_s = staged_plane("xt_s", T, nc.gpsimd)
-        w_s = staged_plane("w_s", R, nc.gpsimd)
-        wb_s = sb("wb_s", N, U8)
-        nc.gpsimd.memset(wb_s[:].bitcast(I32), 0)
+        w2_s = sb("w2_s", R, U8)
+        nc.vector.memset(w2_s[:].bitcast(I32), 0)
 
+        w2_stage = keep.tile([4, 4, R // 4], I32, name="w2_stage")
+        nc.sync.dma_start(w2_stage[:], w2_scales[0].bitcast(I32).rearrange("(q r) n -> r q n", q=4))
         o2 = load_list("o2", offs2)
         xo_w = load_words("xo_w", xo_words[0], Z, U16)
         w2_w = load_words("w2_w", fp8_rows(w2_words), R, U32)
-        w_w = load_words("w_w", w_words[0], R, U16)
-        load_staged(xo_s, xo_scales, Z, nc.scalar)
-        load_staged(w2_s, w2_scales, R, nc.scalar)
+        xo_s = load_plane("xo_s", xo_scales, Z)
         o4 = load_list("o4", offs4)
         o1 = load_list("o1", offs)
-        load_staged(xt_s, xt_scales, T, nc.sync)
-        load_staged(w_s, w_scales, R, nc.sync)
         xt_w = load_words("xt_w", fp8_rows(xt_words), T, U32)
+        w_w = load_words("w_w", w_words[0], R, U16)
+        xt_s = load_plane("xt_s", xt_scales, T)
+        w_s = load_plane("w_s", w_scales, R)
         o3 = load_list("o3", offs3)
         o6 = load_list("o6", offs6)
         o5 = load_list("o5", offs5)
         wb_w = load_words("wb_w", fp8_rows(wb_words), N, U32)
-        for q in range(4):
-            nc.sync.dma_start(wb_s[32 * q : 32 * q + 4, :].bitcast(I32), wb_scales[0, 4 * q : 4 * q + 4, :].bitcast(I32))
+        wb_s = load_plane("wb_s", wb_scales, N)
 
         banks = [psum.tile([P, 512], F32, name=f"bank{i}") for i in range(8)]
 
-        xo_p = unstage("xo_p", xo_s, Z)
-        xo_gs = sb("xo_gs", J, U8)
-        nc.vector.tensor_copy(xo_gs[:], xo_p[:].indirect(o2[:]))
-        lift_upper_half(w2_s, R)
-        w2_ds = deal(nc.vector.tensor_copy, "w2_ds", w2_s[:, 0:R], U8, 16)
+        for q in range(4):
+            nc.vector.tensor_copy(w2_s[32 * q : 32 * q + 4, :].bitcast(I32), w2_stage[:, q, :])
+        w2_ds = deal(nc.vector.tensor_copy, "w2_ds", w2_s[:], U8, 16)
         xo_gw = sb("xo_gw", J, U16)
         nc.vector.tensor_copy(xo_gw[:], xo_w[:].indirect(o2[:]))
+        xo_gs = sb("xo_gs", J, U8)
+        nc.vector.tensor_copy(xo_gs[:], xo_s[:].indirect(o2[:]))
         w2_dw = deal(nc.scalar.copy, "w2_dw", w2_w[:], U32, 4)
-        w_dw = deal(nc.scalar.copy, "w_dw", w_w[:], U16, 8)
 
         pv = [sb(f"pv{t}", C, F32) for t in range(PACK)]
         pw = [sb(f"pw{t}", C, F32) for t in range(PACK)]
         for t in range(PACK):
-            nc.vector.memset(pv[t][:], 0.0)
+            nc.vector.memset(pv[t][:].bitcast(I32), 0)
+            nc.gpsimd.memset(pw[t][:].bitcast(I32), 0)
 
         b_sb = [sb(f"b{t}", J, F32) for t in range(PACK)]
         a_sb = [sb(f"a{t}", J, F32) for t in range(PACK)]
@@ -126,59 +108,66 @@ def tile_list_crossread_twotab_one_plain_kernel(
                 out=banks[t][:, 0:J], lhsT=w2_dw[:, cols].bitcast(E5M2), lhsT_scale=w2_ds[:, cols],
                 rhs=xo_gw[:].bitcast(E2M1), rhs_scale=xo_gs[:], start=True, stop=True,
             )
-        nc.scalar.copy(b_sb[0][:], banks[0][:, 0:J])
+        nc.vector.tensor_copy(b_sb[0][:], banks[0][:, 0:J])
+        nc.vector.tensor_copy(pv[0][:].indirect(o4[:]), b_sb[0][:])
         for t in range(1, PACK):
-            nc.vector.tensor_copy(b_sb[t][:], banks[t][:, 0:J])
-        for t in range(PACK):
+            nc.scalar.copy(b_sb[t][:], banks[t][:, 0:J])
             nc.scalar.activation(out=pv[t][:].indirect(o4[:]), in_=b_sb[t][:], func=COPY)
 
-        xt_p = unstage("xt_p", xt_s, T)
-        xt_gs = sb("xt_gs", J, U8)
-        nc.vector.tensor_copy(xt_gs[:], xt_p[:].indirect(o1[:]))
-        lift_upper_half(w_s, R)
-        w_ds = deal(nc.vector.tensor_copy, "w_ds", w_s[:, 0:R], U8, 16)
         xt_gw = sb("xt_gw", J, U32)
         nc.vector.tensor_copy(xt_gw[:], xt_w[:].indirect(o1[:]))
+        w_dw = deal(nc.vector.tensor_copy, "w_dw", w_w[:], U16, 8)
+        xt_gs = sb("xt_gs", J, U8)
+        nc.vector.tensor_copy(xt_gs[:], xt_s[:].indirect(o1[:]))
+        w_ds = deal(nc.vector.tensor_copy, "w_ds", w_s[:], U8, 16)
         for t in range(PACK):
             cols = slice(P * t, P * (t + 1))
             nc.tensor.matmul_mx(
                 out=banks[PACK + t][:, 0:J], lhsT=w_dw[:, cols].bitcast(E2M1), lhsT_scale=w_ds[:, cols],
                 rhs=xt_gw[:].bitcast(E4M3), rhs_scale=xt_gs[:], start=True, stop=True,
             )
-        for t in range(PACK):
-            nc.vector.memset(pw[t][:], 0.0)
-        for t in range(PACK):
-            nc.vector.tensor_copy(a_sb[t][:], banks[PACK + t][:, 0:J])
+        nc.vector.tensor_copy(a_sb[0][:], banks[PACK][:, 0:J])
         nc.vector.tensor_copy(pw[0][:].indirect(o3[:]), a_sb[0][:])
+        for t in range(1, PACK):
+            nc.scalar.copy(a_sb[t][:], banks[PACK + t][:, 0:J])
         for t in range(1, PACK):
             nc.scalar.activation(out=pw[t][:].indirect(o3[:]), in_=a_sb[t][:], func=COPY)
 
         u = keep.tile([P, PACK, J], F32, name="u", align_bytes=64)
         v = keep.tile([P, PACK, J], F32, name="v", align_bytes=64)
-        for t in range(PACK):
+        nc.vector.tensor_tensor(v[:, 0, :], pv[0][:].indirect(o6[:]), a_sb[0][:], SUB)
+        nc.vector.tensor_tensor(u[:, 0, :], pw[0][:].indirect(o5[:]), b_sb[0][:], SUB)
+        for t in range(1, PACK):
             nc.vector.tensor_tensor(v[:, t, :], pv[t][:].indirect(o6[:]), a_sb[t][:], SUB)
-        for t in range(PACK):
+        for t in range(1, PACK - 1):
             nc.vector.tensor_tensor(u[:, t, :], pw[t][:].indirect(o5[:]), b_sb[t][:], SUB)
+        H = J // 2
+        halves = [slice(H * h, H * (h + 1)) for h in range(2)]
+        for h, js in enumerate(halves):
+            nc.vector.tensor_tensor(u[:, 3, js], pw[3][:].indirect(o5[:, 8 * h : 8 * h + 8]), b_sb[3][:, js], SUB)
 
-        hid = keep.tile([P, J, PACK], BF16, name="hid", align_bytes=64)
-        nc.vector.tensor_tensor(
-            hid[:].rearrange("p (c i) t -> p c t i", i=4),
-            u[:].rearrange("p t (c i) -> p c t i", i=4),
-            v[:].rearrange("p t (c i) -> p c t i", i=4),
-            MAX,
-        )
-        hid_w = sb("hid_w", J, U32)
-        hid_s = sb("hid_s", J, U8)
-        nc.vector.quantize_mx(out=hid_w[:].bitcast(E4M3), scales=hid_s[:], in_=hid[:].rearrange("p j t -> p (j t)"))
-
-        for m in range(N // P):
-            cols = slice(P * m, P * (m + 1))
-            nc.tensor.matmul_mx(
-                out=banks[m][:, 0:J], lhsT=wb_w[:, cols].bitcast(E5M2), lhsT_scale=wb_s[:, cols],
-                rhs=hid_w[:].bitcast(E4M3), rhs_scale=hid_s[:], start=True, stop=True,
+        hid = [keep.tile([P, H, PACK], BF16, name=f"hid{h}", align_bytes=64) for h in range(2)]
+        for h, js in enumerate(halves):
+            nc.vector.tensor_tensor(
+                hid[h][:].rearrange("p (c i) t -> p c t i", i=4),
+                u[:, :, js].rearrange("p t (c i) -> p c t i", i=4),
+                v[:, :, js].rearrange("p t (c i) -> p c t i", i=4),
+                MAX,
             )
-        y = [sb(f"y{m}", J, F32) for m in range(N // P)]
-        nc.scalar.copy(y[0][:], banks[0][:, 0:J])
-        nc.vector.tensor_copy(y[1][:], banks[1][:, 0:J])
-        nc.scalar.dma_start(out[0:P, :], y[0][:])
-        nc.sync.dma_start(out[P : 2 * P, :], y[1][:])
+        hid_w = [sb(f"hid_w{h}", H, U32) for h in range(2)]
+        hid_s = [sb(f"hid_s{h}", H, U8) for h in range(2)]
+        for h in range(2):
+            nc.vector.quantize_mx(out=hid_w[h][:].bitcast(E4M3), scales=hid_s[h][:], in_=hid[h][:].rearrange("p j t -> p (j t)"))
+
+        for h, js in enumerate(halves):
+            for m in range(N // P):
+                cols = slice(P * m, P * (m + 1))
+                nc.tensor.matmul_mx(
+                    out=banks[2 * h + m][:, 0:H], lhsT=wb_w[:, cols].bitcast(E5M2), lhsT_scale=wb_s[:, cols],
+                    rhs=hid_w[h][:].bitcast(E4M3), rhs_scale=hid_s[h][:], start=True, stop=True,
+                )
+            y = [sb(f"y{h}{m}", H, F32) for m in range(N // P)]
+            nc.scalar.copy(y[0][:], banks[2 * h][:, 0:H])
+            nc.vector.tensor_copy(y[1][:], banks[2 * h + 1][:, 0:H])
+            nc.scalar.dma_start(out[0:P, js], y[0][:])
+            nc.sync.dma_start(out[P : 2 * P, js], y[1][:])

@@ -31,8 +31,8 @@ def tile_list_crossread_twotab_one_plain_kernel(
         keep = ctx.enter_context(tc.tile_pool(name="keep", bufs=1))
         psum = ctx.enter_context(tc.psum_pool(name="psum", bufs=1))
 
-        def sb(name, width, dtype):
-            return keep.tile([P, width], dtype, name=name, align_bytes=64)
+        def sb(name, width, dtype, tag=""):
+            return keep.tile([P, width], dtype, name=name, tag=tag or name, align_bytes=64)
 
         def load_list(name, src):
             tile = keep.tile([P, J // 16], U16, name=name)
@@ -72,11 +72,11 @@ def tile_list_crossread_twotab_one_plain_kernel(
         w2_w = load_words("w2_w", fp8_rows(w2_words), R, U32)
         xo_s = load_plane("xo_s", xo_scales, Z)
         o4 = load_list("o4", offs4)
+        w_w = load_words("w_w", w_words[0], R, U16)
+        w_s = load_plane("w_s", w_scales, R)
         o1 = load_list("o1", offs)
         xt_w = load_words("xt_w", fp8_rows(xt_words), T, U32)
-        w_w = load_words("w_w", w_words[0], R, U16)
         xt_s = load_plane("xt_s", xt_scales, T)
-        w_s = load_plane("w_s", w_scales, R)
         o3 = load_list("o3", offs3)
         o6 = load_list("o6", offs6)
         o5 = load_list("o5", offs5)
@@ -93,12 +93,11 @@ def tile_list_crossread_twotab_one_plain_kernel(
         xo_gs = sb("xo_gs", J, U8)
         nc.vector.tensor_copy(xo_gs[:], xo_s[:].indirect(o2[:]))
         w2_dw = deal(nc.scalar.copy, "w2_dw", w2_w[:], U32, 4)
+        w_dw = deal(nc.scalar.copy, "w_dw", w_w[:], U16, 8)
 
         pv = [sb(f"pv{t}", C, F32) for t in range(PACK)]
-        pw = [sb(f"pw{t}", C, F32) for t in range(PACK)]
         for t in range(PACK):
             nc.vector.memset(pv[t][:].bitcast(I32), 0)
-            nc.gpsimd.memset(pw[t][:].bitcast(I32), 0)
 
         b_sb = [sb(f"b{t}", J, F32) for t in range(PACK)]
         a_sb = [sb(f"a{t}", J, F32) for t in range(PACK)]
@@ -114,18 +113,20 @@ def tile_list_crossread_twotab_one_plain_kernel(
             nc.scalar.copy(b_sb[t][:], banks[t][:, 0:J])
             nc.scalar.activation(out=pv[t][:].indirect(o4[:]), in_=b_sb[t][:], func=COPY)
 
+        w_ds = deal(nc.vector.tensor_copy, "w_ds", w_s[:], U8, 16)
         xt_gw = sb("xt_gw", J, U32)
         nc.vector.tensor_copy(xt_gw[:], xt_w[:].indirect(o1[:]))
-        w_dw = deal(nc.vector.tensor_copy, "w_dw", w_w[:], U16, 8)
         xt_gs = sb("xt_gs", J, U8)
         nc.vector.tensor_copy(xt_gs[:], xt_s[:].indirect(o1[:]))
-        w_ds = deal(nc.vector.tensor_copy, "w_ds", w_s[:], U8, 16)
         for t in range(PACK):
             cols = slice(P * t, P * (t + 1))
             nc.tensor.matmul_mx(
                 out=banks[PACK + t][:, 0:J], lhsT=w_dw[:, cols].bitcast(E2M1), lhsT_scale=w_ds[:, cols],
                 rhs=xt_gw[:].bitcast(E4M3), rhs_scale=xt_gs[:], start=True, stop=True,
             )
+        pw = [sb(f"pw{t}", C, F32, tag) for t, tag in enumerate(("xo_s", "xo_gw", "xt_s", "xt_gw"))]
+        for t in range(PACK):
+            nc.vector.memset(pw[t][:].bitcast(I32), 0)
         nc.vector.tensor_copy(a_sb[0][:], banks[PACK][:, 0:J])
         nc.vector.tensor_copy(pw[0][:].indirect(o3[:]), a_sb[0][:])
         for t in range(1, PACK):

@@ -87,11 +87,20 @@ def tile_list_crossread_twotab_one_plain_kernel(
 
         for q in range(4):
             nc.vector.tensor_copy(w2_s[32 * q : 32 * q + 4, :].bitcast(I32), w2_stage[:, q, :])
-        w2_ds = deal(nc.vector.tensor_copy, "w2_ds", w2_s[:], U8, 16)
+        w2_ds = [sb(f"w2_ds{g}", R // 2, U8) for g in range(2)]
+
+        def deal_pair(g):
+            nc.vector.tensor_copy(
+                w2_ds[g][:].rearrange("p (t c i) -> p c t i", t=2, i=16),
+                w2_s[:].rearrange("p (c i t) -> p c t i", t=PACK, i=16)[:, :, 2 * g : 2 * g + 2, :],
+            )
+
+        deal_pair(0)
         xo_gw = sb("xo_gw", J, U16)
         nc.vector.tensor_copy(xo_gw[:], xo_w[:].indirect(o2[:]))
         xo_gs = sb("xo_gs", J, U8)
         nc.vector.tensor_copy(xo_gs[:], xo_s[:].indirect(o2[:]))
+        deal_pair(1)
         w2_dw = deal(nc.scalar.copy, "w2_dw", w2_w[:], U32, 4)
         w_dw = deal(nc.scalar.copy, "w_dw", w_w[:], U16, 8)
 
@@ -104,7 +113,7 @@ def tile_list_crossread_twotab_one_plain_kernel(
         for t in range(PACK):
             cols = slice(P * t, P * (t + 1))
             nc.tensor.matmul_mx(
-                out=banks[t][:, 0:J], lhsT=w2_dw[:, cols].bitcast(E5M2), lhsT_scale=w2_ds[:, cols],
+                out=banks[t][:, 0:J], lhsT=w2_dw[:, cols].bitcast(E5M2), lhsT_scale=w2_ds[t // 2][:, P * (t % 2) : P * (t % 2 + 1)],
                 rhs=xo_gw[:].bitcast(E2M1), rhs_scale=xo_gs[:], start=True, stop=True,
             )
         nc.vector.tensor_copy(b_sb[0][:], banks[0][:, 0:J])
@@ -113,7 +122,7 @@ def tile_list_crossread_twotab_one_plain_kernel(
             nc.scalar.copy(b_sb[t][:], banks[t][:, 0:J])
             nc.scalar.activation(out=pv[t][:].indirect(o4[:]), in_=b_sb[t][:], func=COPY)
 
-        w_ds = deal(nc.vector.tensor_copy, "w_ds", w_s[:], U8, 16)
+        w_ds = deal(nc.gpsimd.tensor_copy, "w_ds", w_s[:], U8, 16)
         xt_gw = sb("xt_gw", J, U32)
         nc.vector.tensor_copy(xt_gw[:], xt_w[:].indirect(o1[:]))
         xt_gs = sb("xt_gs", J, U8)
@@ -124,13 +133,12 @@ def tile_list_crossread_twotab_one_plain_kernel(
                 out=banks[PACK + t][:, 0:J], lhsT=w_dw[:, cols].bitcast(E2M1), lhsT_scale=w_ds[:, cols],
                 rhs=xt_gw[:].bitcast(E4M3), rhs_scale=xt_gs[:], start=True, stop=True,
             )
-        pw = [sb(f"pw{t}", C, F32, tag) for t, tag in enumerate(("xo_s", "xo_gw", "xt_s", "xt_gw"))]
+        pw = [sb(f"pw{t}", C, F32, tag) for t, tag in enumerate(("xo_w", "w2_w", "xo_s", "w2_s"))]
         for t in range(PACK):
-            nc.vector.memset(pw[t][:].bitcast(I32), 0)
-        nc.vector.tensor_copy(a_sb[0][:], banks[PACK][:, 0:J])
+            nc.gpsimd.memset(pw[t][:].bitcast(I32), 0)
+        for t in range(PACK):
+            nc.vector.tensor_copy(a_sb[t][:], banks[PACK + t][:, 0:J])
         nc.vector.tensor_copy(pw[0][:].indirect(o3[:]), a_sb[0][:])
-        for t in range(1, PACK):
-            nc.scalar.copy(a_sb[t][:], banks[PACK + t][:, 0:J])
         for t in range(1, PACK):
             nc.scalar.activation(out=pw[t][:].indirect(o3[:]), in_=a_sb[t][:], func=COPY)
 

@@ -3,7 +3,7 @@ from contextlib import ExitStack
 import concourse.mybir as mybir
 
 K, T, Z, J, R, C, N = 512, 1024, 1024, 256, 512, 512, 256
-FLOPS = 2 * K * R * J * 2 + 2 * R * N * J
+FLOPS = 2 * (2 * K * R * J) + 2 * R * N * J
 
 F32 = mybir.dt.float32
 BF16 = mybir.dt.bfloat16
@@ -20,6 +20,12 @@ MAX = mybir.AluOpType.max
 
 P = 128
 PACK = 4
+QUADRANTS = 4
+SCALE_ROWS = 4
+GROUP = 16
+LINE = 16
+BANK = 512
+H = J // 2
 
 
 def tile_list_crossread_twotab_one_plain_kernel(
@@ -35,7 +41,7 @@ def tile_list_crossread_twotab_one_plain_kernel(
             return keep.tile([P, width], dtype, name=name, tag=tag or name, align_bytes=64)
 
         def load_list(name, src):
-            tile = keep.tile([P, J // 16], U16, name=name)
+            tile = keep.tile([P, J // GROUP], U16, name=name)
             nc.sync.dma_start(tile[:], src)
             return tile
 
@@ -47,14 +53,16 @@ def tile_list_crossread_twotab_one_plain_kernel(
         def fp8_rows(words):
             return words[0].rearrange("p n t -> p (n t)")
 
-        def load_plane(name, scales, n):
-            tile = sb(name, n, U8)
-            for q in range(4):
-                rows = scales[0, 4 * q : 4 * q + 4, :].bitcast(I32)
-                nc.sync.dma_start(tile[32 * q : 32 * q + 32, :].bitcast(I32), rows.unsqueeze(0).to_broadcast([8, 4, n // 4]))
+        def load_plane(name, scales, width):
+            tile = sb(name, width, U8)
+            for q in range(QUADRANTS):
+                rows = scales[0, SCALE_ROWS * q : SCALE_ROWS * (q + 1), :].bitcast(I32)
+                repeated = rows.unsqueeze(0).to_broadcast([32 // SCALE_ROWS, SCALE_ROWS, width // 4])
+                nc.sync.dma_start(tile[32 * q : 32 * (q + 1), :].bitcast(I32), repeated)
             return tile
 
-        def deal(engine_copy, name, src, dtype, run):
+        def deal(engine_copy, name, src, dtype, element_bytes):
+            run = LINE // element_bytes
             tile = sb(name, R, dtype)
             engine_copy(
                 tile[:].rearrange("p (t c i) -> p c t i", t=PACK, i=run),
@@ -64,9 +72,8 @@ def tile_list_crossread_twotab_one_plain_kernel(
 
         w2_s = sb("w2_s", R, U8)
         nc.vector.memset(w2_s[:].bitcast(I32), 0)
-
-        w2_stage = keep.tile([4, 4, R // 4], I32, name="w2_stage")
-        nc.sync.dma_start(w2_stage[:], w2_scales[0].bitcast(I32).rearrange("(q r) n -> r q n", q=4))
+        w2_stage = keep.tile([SCALE_ROWS, QUADRANTS, R // 4], I32, name="w2_stage")
+        nc.sync.dma_start(w2_stage[:], w2_scales[0].bitcast(I32).rearrange("(q i) n -> i q n", q=QUADRANTS))
         o2 = load_list("o2", offs2)
         xo_w = load_words("xo_w", xo_words[0], Z, U16)
         w2_w = load_words("w2_w", fp8_rows(w2_words), R, U32)
@@ -83,26 +90,20 @@ def tile_list_crossread_twotab_one_plain_kernel(
         wb_w = load_words("wb_w", fp8_rows(wb_words), N, U32)
         wb_s = load_plane("wb_s", wb_scales, N)
 
-        banks = [psum.tile([P, 512], F32, name=f"bank{i}") for i in range(8)]
+        banks = [psum.tile([P, BANK], F32, name=f"bank{i}") for i in range(8)]
+        whole = slice(0, J)
+        halves = [slice(H * h, H * (h + 1)) for h in range(2)]
+        list_halves = [slice(H // GROUP * h, H // GROUP * (h + 1)) for h in range(2)]
 
-        for q in range(4):
-            nc.vector.tensor_copy(w2_s[32 * q : 32 * q + 4, :].bitcast(I32), w2_stage[:, q, :])
-        w2_ds = [sb(f"w2_ds{g}", R // 2, U8) for g in range(2)]
-
-        def deal_pair(g):
-            nc.vector.tensor_copy(
-                w2_ds[g][:].rearrange("p (t c i) -> p c t i", t=2, i=16),
-                w2_s[:].rearrange("p (c i t) -> p c t i", t=PACK, i=16)[:, :, 2 * g : 2 * g + 2, :],
-            )
-
-        deal_pair(0)
+        for q in range(QUADRANTS):
+            nc.vector.tensor_copy(w2_s[32 * q : 32 * q + SCALE_ROWS, :].bitcast(I32), w2_stage[:, q, :])
+        w2_ds = deal(nc.vector.tensor_copy, "w2_ds", w2_s[:], U8, 1)
         xo_gw = sb("xo_gw", J, U16)
         nc.vector.tensor_copy(xo_gw[:], xo_w[:].indirect(o2[:]))
         xo_gs = sb("xo_gs", J, U8)
-        nc.vector.tensor_copy(xo_gs[:], xo_s[:].indirect(o2[:]))
-        deal_pair(1)
+        for js, ls in zip(halves, list_halves):
+            nc.vector.tensor_copy(xo_gs[:, js], xo_s[:].indirect(o2[:, ls]))
         w2_dw = deal(nc.scalar.copy, "w2_dw", w2_w[:], U32, 4)
-        w_dw = deal(nc.scalar.copy, "w_dw", w_w[:], U16, 8)
 
         pv = [sb(f"pv{t}", C, F32) for t in range(PACK)]
         for t in range(PACK):
@@ -110,73 +111,98 @@ def tile_list_crossread_twotab_one_plain_kernel(
 
         b_sb = [sb(f"b{t}", J, F32) for t in range(PACK)]
         a_sb = [sb(f"a{t}", J, F32) for t in range(PACK)]
-        for t in range(PACK):
+
+        def product_b(bank, t, js):
             cols = slice(P * t, P * (t + 1))
             nc.tensor.matmul_mx(
-                out=banks[t][:, 0:J], lhsT=w2_dw[:, cols].bitcast(E5M2), lhsT_scale=w2_ds[t // 2][:, P * (t % 2) : P * (t % 2 + 1)],
-                rhs=xo_gw[:].bitcast(E2M1), rhs_scale=xo_gs[:], start=True, stop=True,
+                out=bank[:, js], lhsT=w2_dw[:, cols].bitcast(E5M2), lhsT_scale=w2_ds[:, cols],
+                rhs=xo_gw[:, js].bitcast(E2M1), rhs_scale=xo_gs[:, js], start=True, stop=True,
             )
-        nc.vector.tensor_copy(b_sb[0][:], banks[0][:, 0:J])
-        nc.vector.tensor_copy(pv[0][:].indirect(o4[:]), b_sb[0][:])
-        for t in range(1, PACK):
-            nc.scalar.copy(b_sb[t][:], banks[t][:, 0:J])
+
+        for h, js in enumerate(halves):
+            product_b(banks[2 * h], 1, js)
+            product_b(banks[2 * h + 1], 0, js)
+        for t in range(2, PACK):
+            product_b(banks[2 + t], t, whole)
+        for h, (js, ls) in enumerate(zip(halves, list_halves)):
+            nc.scalar.copy(b_sb[1][:, js], banks[2 * h][:, js])
+            nc.scalar.activation(out=pv[1][:].indirect(o4[:, ls]), in_=b_sb[1][:, js], func=COPY)
+            nc.vector.tensor_copy(b_sb[0][:, js], banks[2 * h + 1][:, js])
+            nc.vector.tensor_copy(pv[0][:].indirect(o4[:, ls]), b_sb[0][:, js])
+        for t in range(2, PACK):
+            nc.scalar.copy(b_sb[t][:], banks[2 + t][:, whole])
             nc.scalar.activation(out=pv[t][:].indirect(o4[:]), in_=b_sb[t][:], func=COPY)
 
-        w_ds = deal(nc.gpsimd.tensor_copy, "w_ds", w_s[:], U8, 16)
+        w_ds = deal(nc.gpsimd.tensor_copy, "w_ds", w_s[:], U8, 1)
+        w_dw = deal(nc.vector.tensor_copy, "w_dw", w_w[:], U16, 2)
         xt_gw = sb("xt_gw", J, U32)
         nc.vector.tensor_copy(xt_gw[:], xt_w[:].indirect(o1[:]))
         xt_gs = sb("xt_gs", J, U8)
-        nc.vector.tensor_copy(xt_gs[:], xt_s[:].indirect(o1[:]))
-        for t in range(PACK):
+        for js, ls in zip(halves, list_halves):
+            nc.vector.tensor_copy(xt_gs[:, js], xt_s[:].indirect(o1[:, ls]))
+
+        def product_a(bank, t, js):
             cols = slice(P * t, P * (t + 1))
             nc.tensor.matmul_mx(
-                out=banks[PACK + t][:, 0:J], lhsT=w_dw[:, cols].bitcast(E2M1), lhsT_scale=w_ds[:, cols],
-                rhs=xt_gw[:].bitcast(E4M3), rhs_scale=xt_gs[:], start=True, stop=True,
+                out=bank[:, js], lhsT=w_dw[:, cols].bitcast(E2M1), lhsT_scale=w_ds[:, cols],
+                rhs=xt_gw[:, js].bitcast(E4M3), rhs_scale=xt_gs[:, js], start=True, stop=True,
             )
-        pw = [sb(f"pw{t}", C, F32, tag) for t, tag in enumerate(("xo_w", "w2_w", "xo_s", "w2_s"))]
+
+        for h, js in enumerate(halves):
+            product_a(banks[6 + h], 0, js)
+        for t in range(1, PACK):
+            product_a(banks[t - 1], t, whole)
+
+        pw = [sb(f"pw{t}", C, F32, tag) for t, tag in enumerate(("w2_s", "xo_w", "w2_w", "xo_s"))]
         for t in range(PACK):
             nc.gpsimd.memset(pw[t][:].bitcast(I32), 0)
-        for t in range(PACK):
-            nc.vector.tensor_copy(a_sb[t][:], banks[PACK + t][:, 0:J])
-        nc.vector.tensor_copy(pw[0][:].indirect(o3[:]), a_sb[0][:])
+
+        nc.vector.tensor_copy(a_sb[0][:, halves[0]], banks[6][:, halves[0]])
+        nc.vector.tensor_copy(pw[0][:].indirect(o3[:, list_halves[0]]), a_sb[0][:, halves[0]])
+        nc.vector.tensor_copy(a_sb[0][:, halves[1]], banks[7][:, halves[1]])
+        for t in range(1, PACK):
+            nc.vector.tensor_copy(a_sb[t][:], banks[t - 1][:, whole])
+        nc.vector.tensor_copy(pw[0][:].indirect(o3[:, list_halves[1]]), a_sb[0][:, halves[1]])
         for t in range(1, PACK):
             nc.scalar.activation(out=pw[t][:].indirect(o3[:]), in_=a_sb[t][:], func=COPY)
 
         u = keep.tile([P, PACK, J], F32, name="u", align_bytes=64)
         v = keep.tile([P, PACK, J], F32, name="v", align_bytes=64)
+        last = PACK - 1
         nc.vector.tensor_tensor(v[:, 0, :], pv[0][:].indirect(o6[:]), a_sb[0][:], SUB)
         nc.vector.tensor_tensor(u[:, 0, :], pw[0][:].indirect(o5[:]), b_sb[0][:], SUB)
         for t in range(1, PACK):
             nc.vector.tensor_tensor(v[:, t, :], pv[t][:].indirect(o6[:]), a_sb[t][:], SUB)
-        for t in range(1, PACK - 1):
+        for t in range(1, last):
             nc.vector.tensor_tensor(u[:, t, :], pw[t][:].indirect(o5[:]), b_sb[t][:], SUB)
-        H = J // 2
-        halves = [slice(H * h, H * (h + 1)) for h in range(2)]
-        for h, js in enumerate(halves):
-            nc.vector.tensor_tensor(u[:, 3, js], pw[3][:].indirect(o5[:, 8 * h : 8 * h + 8]), b_sb[3][:, js], SUB)
+        for js, ls in zip(halves, list_halves):
+            nc.vector.tensor_tensor(u[:, last, js], pw[last][:].indirect(o5[:, ls]), b_sb[last][:, js], SUB)
 
+        line_slots = LINE // 4
         hid = [keep.tile([P, H, PACK], BF16, name=f"hid{h}", align_bytes=64) for h in range(2)]
         for h, js in enumerate(halves):
             nc.vector.tensor_tensor(
-                hid[h][:].rearrange("p (c i) t -> p c t i", i=4),
-                u[:, :, js].rearrange("p t (c i) -> p c t i", i=4),
-                v[:, :, js].rearrange("p t (c i) -> p c t i", i=4),
+                hid[h][:].rearrange("p (c i) t -> p c t i", i=line_slots),
+                u[:, :, js].rearrange("p t (c i) -> p c t i", i=line_slots),
+                v[:, :, js].rearrange("p t (c i) -> p c t i", i=line_slots),
                 MAX,
             )
         hid_w = [sb(f"hid_w{h}", H, U32) for h in range(2)]
         hid_s = [sb(f"hid_s{h}", H, U8) for h in range(2)]
         for h in range(2):
-            nc.vector.quantize_mx(out=hid_w[h][:].bitcast(E4M3), scales=hid_s[h][:], in_=hid[h][:].rearrange("p j t -> p (j t)"))
+            nc.vector.quantize_mx(
+                out=hid_w[h][:].bitcast(E4M3), scales=hid_s[h][:], in_=hid[h][:].rearrange("p j t -> p (j t)")
+            )
 
         for h, js in enumerate(halves):
             for m in range(N // P):
                 cols = slice(P * m, P * (m + 1))
                 nc.tensor.matmul_mx(
-                    out=banks[2 * h + m][:, 0:H], lhsT=wb_w[:, cols].bitcast(E5M2), lhsT_scale=wb_s[:, cols],
+                    out=banks[4 + 2 * h + m][:, 0:H], lhsT=wb_w[:, cols].bitcast(E5M2), lhsT_scale=wb_s[:, cols],
                     rhs=hid_w[h][:].bitcast(E4M3), rhs_scale=hid_s[h][:], start=True, stop=True,
                 )
             y = [sb(f"y{h}{m}", H, F32) for m in range(N // P)]
-            nc.scalar.copy(y[0][:], banks[2 * h][:, 0:H])
-            nc.vector.tensor_copy(y[1][:], banks[2 * h + 1][:, 0:H])
+            nc.scalar.copy(y[0][:], banks[4 + 2 * h][:, 0:H])
+            nc.vector.tensor_copy(y[1][:], banks[5 + 2 * h][:, 0:H])
             nc.scalar.dma_start(out[0:P, js], y[0][:])
             nc.sync.dma_start(out[P : 2 * P, js], y[1][:])

from contextlib import ExitStack

import concourse.mybir as mybir

K, T, Z, J, R, C, N = 512, 1024, 1024, 256, 512, 512, 256
FLOPS = 2 * (2 * K * R * J) + 2 * R * N * J

F32 = mybir.dt.float32
BF16 = mybir.dt.bfloat16
I32 = mybir.dt.int32
U32 = mybir.dt.uint32
U16 = mybir.dt.uint16
U8 = mybir.dt.uint8
E4M3 = mybir.dt.float8_e4m3fn_x4
E5M2 = mybir.dt.float8_e5m2_x4
E2M1 = mybir.dt.float4_e2m1fn_x4
COPY = mybir.ActivationFunctionType.Copy
SUB = mybir.AluOpType.subtract
MAX = mybir.AluOpType.max

P = 128
PACK = 4
QUADRANTS = 4
SCALE_ROWS = 4
GROUP = 16
LINE = 16
BANK = 512
H = J // 2


def tile_list_crossread_twotab_one_plain_kernel(
    tc, xt_words, xt_scales, w_words, w_scales, xo_words, xo_scales, w2_words, w2_scales,
    wb_words, wb_scales, offs, offs2, offs3, offs4, offs5, offs6, out,
):
    nc = tc.nc
    with ExitStack() as ctx:
        keep = ctx.enter_context(tc.tile_pool(name="keep", bufs=1))
        psum = ctx.enter_context(tc.psum_pool(name="psum", bufs=1))

        def sb(name, width, dtype, tag=""):
            return keep.tile([P, width], dtype, name=name, tag=tag or name, align_bytes=64)

        def load_list(name, src):
            tile = keep.tile([P, J // GROUP], U16, name=name)
            nc.sync.dma_start(tile[:], src)
            return tile

        def load_words(name, src, width, dtype):
            tile = sb(name, width, dtype)
            nc.sync.dma_start(tile[:].bitcast(I32), src.bitcast(I32))
            return tile

        def fp8_rows(words):
            return words[0].rearrange("p n t -> p (n t)")

        def load_plane(name, scales, width):
            tile = sb(name, width, U8)
            for q in range(QUADRANTS):
                rows = scales[0, SCALE_ROWS * q : SCALE_ROWS * (q + 1), :].bitcast(I32)
                repeated = rows.unsqueeze(0).to_broadcast([32 // SCALE_ROWS, SCALE_ROWS, width // 4])
                nc.sync.dma_start(tile[32 * q : 32 * (q + 1), :].bitcast(I32), repeated)
            return tile

        def deal(engine_copy, name, src, dtype, element_bytes):
            run = LINE // element_bytes
            tile = sb(name, R, dtype)
            engine_copy(
                tile[:].rearrange("p (t c i) -> p c t i", t=PACK, i=run),
                src.rearrange("p (c i t) -> p c t i", t=PACK, i=run),
            )
            return tile

        w2_s = sb("w2_s", R, U8)
        nc.vector.memset(w2_s[:].bitcast(I32), 0)
        w2_stage = keep.tile([SCALE_ROWS, QUADRANTS, R // 4], I32, name="w2_stage")
        nc.sync.dma_start(w2_stage[:], w2_scales[0].bitcast(I32).rearrange("(q i) n -> i q n", q=QUADRANTS))
        o2 = load_list("o2", offs2)
        xo_w = load_words("xo_w", xo_words[0], Z, U16)
        w2_w = load_words("w2_w", fp8_rows(w2_words), R, U32)
        xo_s = load_plane("xo_s", xo_scales, Z)
        o4 = load_list("o4", offs4)
        w_w = load_words("w_w", w_words[0], R, U16)
        w_s = load_plane("w_s", w_scales, R)
        o1 = load_list("o1", offs)
        xt_w = load_words("xt_w", fp8_rows(xt_words), T, U32)
        xt_s = load_plane("xt_s", xt_scales, T)
        o3 = load_list("o3", offs3)
        o6 = load_list("o6", offs6)
        o5 = load_list("o5", offs5)
        wb_w = load_words("wb_w", fp8_rows(wb_words), N, U32)
        wb_s = load_plane("wb_s", wb_scales, N)

        banks = [psum.tile([P, BANK], F32, name=f"bank{i}") for i in range(8)]
        whole = slice(0, J)
        halves = [slice(H * h, H * (h + 1)) for h in range(2)]
        list_halves = [slice(H // GROUP * h, H // GROUP * (h + 1)) for h in range(2)]

        for q in range(QUADRANTS):
            nc.vector.tensor_copy(w2_s[32 * q : 32 * q + SCALE_ROWS, :].bitcast(I32), w2_stage[:, q, :])
        w2_ds = deal(nc.vector.tensor_copy, "w2_ds", w2_s[:], U8, 1)
        xo_gw = sb("xo_gw", J, U16)
        nc.vector.tensor_copy(xo_gw[:], xo_w[:].indirect(o2[:]))
        xo_gs = sb("xo_gs", J, U8)
        for js, ls in zip(halves, list_halves):
            nc.vector.tensor_copy(xo_gs[:, js], xo_s[:].indirect(o2[:, ls]))
        w2_dw = deal(nc.scalar.copy, "w2_dw", w2_w[:], U32, 4)

        pv = [sb(f"pv{t}", C, F32) for t in range(PACK)]
        for t in range(PACK):
            nc.vector.memset(pv[t][:].bitcast(I32), 0)

        b_sb = [sb(f"b{t}", J, F32) for t in range(PACK)]
        a_sb = [sb(f"a{t}", J, F32) for t in range(PACK)]

        def product_b(bank, t, js):
            cols = slice(P * t, P * (t + 1))
            nc.tensor.matmul_mx(
                out=bank[:, js], lhsT=w2_dw[:, cols].bitcast(E5M2), lhsT_scale=w2_ds[:, cols],
                rhs=xo_gw[:, js].bitcast(E2M1), rhs_scale=xo_gs[:, js], start=True, stop=True,
            )

        for h, js in enumerate(halves):
            product_b(banks[2 * h], 1, js)
            product_b(banks[2 * h + 1], 0, js)
        for t in range(2, PACK):
            product_b(banks[2 + t], t, whole)
        for h, (js, ls) in enumerate(zip(halves, list_halves)):
            nc.scalar.copy(b_sb[1][:, js], banks[2 * h][:, js])
            nc.scalar.activation(out=pv[1][:].indirect(o4[:, ls]), in_=b_sb[1][:, js], func=COPY)
            nc.vector.tensor_copy(b_sb[0][:, js], banks[2 * h + 1][:, js])
            nc.vector.tensor_copy(pv[0][:].indirect(o4[:, ls]), b_sb[0][:, js])
        for t in range(2, PACK):
            nc.scalar.copy(b_sb[t][:], banks[2 + t][:, whole])
            nc.scalar.activation(out=pv[t][:].indirect(o4[:]), in_=b_sb[t][:], func=COPY)

        w_ds = deal(nc.gpsimd.tensor_copy, "w_ds", w_s[:], U8, 1)
        w_dw = deal(nc.vector.tensor_copy, "w_dw", w_w[:], U16, 2)
        xt_gw = sb("xt_gw", J, U32)
        nc.vector.tensor_copy(xt_gw[:], xt_w[:].indirect(o1[:]))
        xt_gs = sb("xt_gs", J, U8)
        for js, ls in zip(halves, list_halves):
            nc.vector.tensor_copy(xt_gs[:, js], xt_s[:].indirect(o1[:, ls]))

        def product_a(bank, t, js):
            cols = slice(P * t, P * (t + 1))
            nc.tensor.matmul_mx(
                out=bank[:, js], lhsT=w_dw[:, cols].bitcast(E2M1), lhsT_scale=w_ds[:, cols],
                rhs=xt_gw[:, js].bitcast(E4M3), rhs_scale=xt_gs[:, js], start=True, stop=True,
            )

        for h, js in enumerate(halves):
            product_a(banks[6 + h], 0, js)
        for t in range(1, PACK):
            product_a(banks[t - 1], t, whole)

        pw = [sb(f"pw{t}", C, F32, tag) for t, tag in enumerate(("w2_s", "xo_w", "w2_w", "xo_s"))]
        for t in range(PACK):
            nc.gpsimd.memset(pw[t][:].bitcast(I32), 0)

        nc.vector.tensor_copy(a_sb[0][:, halves[0]], banks[6][:, halves[0]])
        nc.vector.tensor_copy(pw[0][:].indirect(o3[:, list_halves[0]]), a_sb[0][:, halves[0]])
        nc.vector.tensor_copy(a_sb[0][:, halves[1]], banks[7][:, halves[1]])
        for t in range(1, PACK):
            nc.vector.tensor_copy(a_sb[t][:], banks[t - 1][:, whole])
        nc.vector.tensor_copy(pw[0][:].indirect(o3[:, list_halves[1]]), a_sb[0][:, halves[1]])
        for t in range(1, PACK):
            nc.scalar.activation(out=pw[t][:].indirect(o3[:]), in_=a_sb[t][:], func=COPY)

        u = keep.tile([P, PACK, J], F32, name="u", align_bytes=64)
        v = keep.tile([P, PACK, J], F32, name="v", align_bytes=64)
        last = PACK - 1
        nc.vector.tensor_tensor(v[:, 0, :], pv[0][:].indirect(o6[:]), a_sb[0][:], SUB)
        nc.vector.tensor_tensor(u[:, 0, :], pw[0][:].indirect(o5[:]), b_sb[0][:], SUB)
        for t in range(1, PACK):
            nc.vector.tensor_tensor(v[:, t, :], pv[t][:].indirect(o6[:]), a_sb[t][:], SUB)
        for t in range(1, last):
            nc.vector.tensor_tensor(u[:, t, :], pw[t][:].indirect(o5[:]), b_sb[t][:], SUB)
        for js, ls in zip(halves, list_halves):
            nc.vector.tensor_tensor(u[:, last, js], pw[last][:].indirect(o5[:, ls]), b_sb[last][:, js], SUB)

        line_slots = LINE // 4
        hid = [keep.tile([P, H, PACK], BF16, name=f"hid{h}", align_bytes=64) for h in range(2)]
        for h, js in enumerate(halves):
            nc.vector.tensor_tensor(
                hid[h][:].rearrange("p (c i) t -> p c t i", i=line_slots),
                u[:, :, js].rearrange("p t (c i) -> p c t i", i=line_slots),
                v[:, :, js].rearrange("p t (c i) -> p c t i", i=line_slots),
                MAX,
            )
        hid_w = [sb(f"hid_w{h}", H, U32) for h in range(2)]
        hid_s = [sb(f"hid_s{h}", H, U8) for h in range(2)]
        for h in range(2):
            nc.vector.quantize_mx(
                out=hid_w[h][:].bitcast(E4M3), scales=hid_s[h][:], in_=hid[h][:].rearrange("p j t -> p (j t)")
            )

        for h, js in enumerate(halves):
            for m in range(N // P):
                cols = slice(P * m, P * (m + 1))
                nc.tensor.matmul_mx(
                    out=banks[4 + 2 * h + m][:, 0:H], lhsT=wb_w[:, cols].bitcast(E5M2), lhsT_scale=wb_s[:, cols],
                    rhs=hid_w[h][:].bitcast(E4M3), rhs_scale=hid_s[h][:], start=True, stop=True,
                )
            y = [sb(f"y{h}{m}", H, F32) for m in range(N // P)]
            nc.scalar.copy(y[0][:], banks[4 + 2 * h][:, 0:H])
            nc.vector.tensor_copy(y[1][:], banks[5 + 2 * h][:, 0:H])
            nc.scalar.dma_start(out[0:P, js], y[0][:])
            nc.sync.dma_start(out[P : 2 * P, js], y[1][:])
